import numpy as np
import ml_dtypes


def mxq(x, axis, fmt="e4m3"):
    dtype, down = {"e4m3": (ml_dtypes.float8_e4m3fn, 7), "e5m2": (ml_dtypes.float8_e5m2, 14)}[fmt]
    v = np.moveaxis(np.asarray(x, np.float32).astype(ml_dtypes.bfloat16).astype(np.float64), axis, -1)
    blocks = v.reshape(v.shape[:-1] + (-1, 32))
    amax = np.abs(blocks).max(-1, keepdims=True)
    byte = np.maximum(np.where(amax > 0, np.frexp(amax)[1] - 1 + 127, 0) - down, 1)
    scale = np.exp2(byte - 127.0)
    codes = (blocks / scale).astype(np.float32).astype(dtype).astype(np.float64)
    return np.moveaxis((codes * scale).reshape(v.shape), -1, axis)


WIDE = False


def mx_kscale(k):
    if not WIDE:
        return np.ones(k)
    levels = np.array([10, -10, 5, -5, 0])
    if k % 512:
        return np.exp2(np.random.permutation(np.resize(levels, k // 32))).repeat(32)
    a = np.empty((k // 512, 16))
    for p in range(k // 512):
        a[p, :8] = np.random.permutation(np.resize(levels, 8))
        for g in range(8):
            far = levels[np.abs(levels - a[p, g]) >= 10]
            a[p, g + 8] = far[np.random.randint(len(far))]
    return np.exp2(a.ravel()).repeat(32)


def f64(x):
    return np.asarray(x).astype(np.float64)


def striped(idx):
    return np.tile(idx.reshape(-1, 16).T, (8, 1)).astype(np.uint16)


def unstriped(offs):
    return offs[:16].T.reshape(-1).astype(np.int64)


def striped8(idx):
    return np.concatenate([x.reshape(-1, 16).T for x in idx]).astype(np.uint16)


def runs(offs, k):
    lists = np.stack([offs[16 * r : 16 * r + 16].T.reshape(-1) for r in range(8)]).astype(np.int64)
    return lists[np.arange(k) % 512 // 64]


def pack_weight(w):
    k, n = w.shape
    w = f64(np.asarray(w, np.float32).astype(ml_dtypes.bfloat16)).reshape(k // 32, 32, n)
    amax = np.abs(w).max(1)
    byte = np.clip(np.where(amax > 0, np.frexp(amax)[1] - 1 + 127 - 7, 1), 1, 254)
    scaled = (w * np.exp2(127.0 - byte)[:, None, :]).reshape(k, n).astype(np.float32)
    words = np.ascontiguousarray(scaled.reshape(k // 512, 128, 4, n).transpose(0, 1, 3, 2)).astype(ml_dtypes.float8_e4m3fn).view(np.uint8)
    return words, np.ascontiguousarray(byte.astype(np.uint8).reshape(k // 512, 16, n))


def unpack_weight(words, scales):
    g, p, n, _ = words.shape
    vals = np.ascontiguousarray(words).view(ml_dtypes.float8_e4m3fn).astype(np.float64) * np.repeat(np.exp2(scales.astype(np.float64) - 127.0), 8, axis=1)[..., None]
    return vals.transpose(0, 1, 3, 2).reshape(g * 512, n)


K, T, S, N, H = 512, 2048, 512, 512, 512


def setup_inputs():
    n = np.random.standard_normal
    s = mx_kscale(K)[:, None]
    u = mx_kscale(H)
    packed_xT = pack_weight(n((K, T)) * s)
    return {
        "x_words": packed_xT[0],
        "x_scales": packed_xT[1],
        "w1": (n((K, H)) / np.sqrt(K) / s).astype(np.float32),
        "gn": (np.random.uniform(0.5, 1.5, (H, 1)) * u[:, None]).astype(np.float32),
        "w2": (n((H, N)) / np.sqrt(2 * H) / u[:, None]).astype(np.float32),
        "w3": (n((K, N)) / np.sqrt(2 * K) / s).astype(np.float32),
        "offs": striped(np.random.permutation(T)[:S]),
        "n1": striped8(np.stack([np.random.permutation(S) for _ in range(8)])),
        "n2": striped8(np.stack([np.random.permutation(S) for _ in range(8)])),
        "n3": striped8(np.stack([np.random.permutation(S) for _ in range(8)])),
        "two": striped(np.random.permutation(T)[:S]),
        "n4": striped8(np.stack([np.random.permutation(S) for _ in range(8)])),
        "n5": striped8(np.stack([np.random.permutation(S) for _ in range(8)])),
    }


def reference(x_words, x_scales, w1, gn, w2, w3, offs, n1, n2, n3, two, n4, n5):
    xq = unpack_weight(x_words, x_scales)[:, unstriped(offs)]
    y = mxq(f64(w1), 0, "e4m3").T @ xq
    z = f64(gn) * (np.maximum(y, y[np.arange(H)[:, None], runs(n1, H)]) - (np.maximum(y[np.arange(H)[:, None], runs(n2, H)], y[np.arange(H)[:, None], runs(n3, H)])))
    x_two = unpack_weight(x_words, x_scales)[:, unstriped(two)]
    h = mxq(f64(w2), 0, "e4m3").T @ mxq(z, 0, "e4m3") + mxq(f64(w3), 0, "e4m3").T @ x_two
    return np.minimum(np.maximum(h, h[np.arange(N)[:, None], runs(n4, N)]), h[np.arange(N)[:, None], runs(n5, N)])

@@ -1,0 +1,190 @@
+from contextlib import ExitStack
+
+import concourse.mybir as mybir
+
+K, T, S, H, N = 512, 2048, 512, 512, 512
+FLOPS = 2 * S * (K * H + H * N + K * N)
+
+F32 = mybir.dt.float32
+BF16 = mybir.dt.bfloat16
+I32 = mybir.dt.int32
+U32 = mybir.dt.uint32
+U16 = mybir.dt.uint16
+U8 = mybir.dt.uint8
+FP8X4 = mybir.dt.float8_e4m3fn_x4
+ALU = mybir.AluOpType
+COPY = mybir.ActivationFunctionType.Copy
+
+P = 128
+PACK = 4
+CHUNKS = ((0, 256), (256, 512))
+LOWER_ENDS = ({3: 0}, {2: 0, 3: 3})
+V_FIRST = {(0, 0, 0), (0, 1, 0), (0, 2, 0), (0, 3, 0), (1, 0, 0)}
+V_SECOND = {(0, 0, 0), (0, 0, 1), (1, 0, 0), (1, 0, 1), (0, 1, 0)}
+
+
+def tile_picked_mixinmixminmx_none_p_kernel(
+    tc, x_words, x_scales, w1, gn, w2, w3, offs, n1, n2, n3, two, n4, n5, out
+):
+    nc = tc.nc
+    with ExitStack() as ctx:
+        keep = ctx.enter_context(tc.tile_pool(name="keep", bufs=1))
+        psum = ctx.enter_context(tc.psum_pool(name="psum", bufs=1))
+
+        def load_list(name, src):
+            tile = keep.tile([P, S // 16], U16, name=name)
+            nc.sync.dma_start(tile[:], src)
+            return tile
+
+        def load_weight(name, src):
+            tile = keep.tile([P, PACK, 512], F32, name=name)
+            nc.sync.dma_start(tile[:], src.rearrange("(p j) c -> p j c", j=PACK))
+            return tile
+
+        def gather(on_vector, dst, window, offsets):
+            if on_vector:
+                nc.vector.tensor_copy(dst, window.indirect(offsets))
+            else:
+                nc.scalar.activation(dst, window.indirect(offsets), COPY)
+
+        def quantize(name, grouped, width):
+            codes = keep.tile([P, width], U32, name=name + "_codes", align_bytes=64)
+            scales = keep.tile([P, width], U8, name=name + "_scales", align_bytes=64)
+            nc.vector.quantize_mx(out=codes[:].bitcast(FP8X4), scales=scales[:], in_=grouped)
+            return codes, scales
+
+        x_bytes = keep.tile([P, T], U8, name="x_bytes")
+        nc.vector.memset(x_bytes[:].bitcast(I32), 0)
+        offs_t = load_list("offs_t", offs)
+        two_t = load_list("two_t", two)
+        gain = keep.tile([P, PACK], F32, name="gain")
+        nc.sync.dma_start(gain[:], gn.rearrange("(p t) o -> p (t o)", t=PACK))
+        w1_raw = load_weight("w1_raw", w1)
+        for r in range(4):
+            nc.scalar.dma_start(x_bytes[r:P:32, :].bitcast(I32), x_scales[0, r:16:4, :].bitcast(I32))
+        x_tab = keep.tile([P, T], I32, name="x_tab")
+        nc.sync.dma_start(x_tab[:], x_words[0].rearrange("p n r -> p (n r)").bitcast(I32))
+        first_lists = [load_list("n1_t", n1), load_list("n2_t", n2), load_list("n3_t", n3)]
+        w3_raw = load_weight("w3_raw", w3)
+        w2_raw = load_weight("w2_raw", w2)
+        second_lists = [load_list("n4_t", n4), load_list("n5_t", n5)]
+
+        xa_scales = keep.tile([P, S], U8, name="xa_scales", align_bytes=64)
+        nc.vector.tensor_copy(xa_scales[:], x_bytes[:].indirect(offs_t[:]))
+        xb_scales = keep.tile([P, S], U8, name="xb_scales", align_bytes=64)
+        nc.vector.tensor_copy(xb_scales[:], x_bytes[:].indirect(two_t[:]))
+
+        half = keep.tile([P, PACK], F32, name="half")
+        nc.vector.tensor_scalar(half[:], gain[:], 0.0, 2.0, ALU.is_ge, ALU.mult)
+        sign = keep.tile([P, PACK], F32, name="sign")
+        nc.vector.tensor_scalar(sign[:], half[:], -1.0, None, ALU.add)
+        size = keep.tile([P, PACK], F32, name="size")
+        nc.vector.tensor_tensor(size[:], gain[:], sign[:], ALU.mult)
+
+        w1_q = []
+        w1_view = w1_raw[:].rearrange("p j (m t) -> p m j t", t=PACK)
+        w1_grouped = []
+        for u in range(2):
+            grouped = keep.tile([P, 2 * P * PACK], BF16, name="w1_grouped%d" % u, align_bytes=64)
+            dst = grouped[:].rearrange("p (t m j) -> p m j t", t=2, j=PACK)
+            if u == 0:
+                nc.vector.tensor_copy(dst, w1_view[:, :, :, 0:2])
+            else:
+                nc.scalar.copy(dst, w1_view[:, :, :, 2:4])
+            w1_grouped.append(grouped)
+        for u in range(2):
+            w1_q.append(quantize("w1_%d" % u, w1_grouped[u][:], 2 * P))
+
+        xa_words = keep.tile([P, S], U32, name="xa_words", align_bytes=64)
+        nc.vector.tensor_copy(xa_words[:], x_tab[:].bitcast(U32).indirect(offs_t[:]))
+        xb_words = keep.tile([P, S], U32, name="xb_words", align_bytes=64)
+        nc.vector.tensor_copy(xb_words[:], x_tab[:].bitcast(U32).indirect(two_t[:]))
+
+        y_win = []
+        for t in range(PACK):
+            acc = psum.tile([P, S], F32, name="bank%d" % t, tag="bank%d" % t)
+            codes, scales = w1_q[t // 2]
+            cols = slice((t % 2) * P, (t % 2 + 1) * P)
+            nc.tensor.matmul_mx(out=acc[:], lhsT=codes[:, cols].bitcast(FP8X4), lhsT_scale=scales[:, cols],
+                                rhs=xa_words[:].bitcast(FP8X4), rhs_scale=xa_scales[:], start=True, stop=True)
+            win = keep.tile([P, S], F32, name="y_win%d" % t)
+            nc.scalar.activation(win[:], acc[:], COPY, scale=size[:, t : t + 1])
+            y_win.append(win)
+
+        w32_grouped = keep.tile([P, 2, 512 * PACK], BF16, name="w32_grouped", align_bytes=64)
+        nc.vector.tensor_copy(
+            w32_grouped[:, 0, :].rearrange("p (t m j) -> p m j t", t=PACK, j=PACK),
+            w3_raw[:].rearrange("p j (m t) -> p m j t", t=PACK),
+        )
+        got = [[keep.tile([P, PACK, hi - lo], F32, name="got%d_%d" % (c, i)) for i in range(3)] for c, (lo, hi) in enumerate(CHUNKS)]
+        upper0 = keep.tile([P, PACK, CHUNKS[0][1]], F32, name="upper0")
+        uppers = [upper0[:], w32_grouped[:, 0, :].bitcast(F32).rearrange("p (t w) -> p t w", t=PACK)]
+
+        def upper_part(c, t):
+            lo, hi = CHUNKS[c]
+            gather((c, t, 0) in V_FIRST, got[c][0][:, t, :], y_win[t][:], first_lists[0][:, lo // 16 : hi // 16])
+            nc.vector.tensor_tensor(uppers[c][:, t, :], y_win[t][:, lo:hi], got[c][0][:, t, :], ALU.max)
+
+        for t in range(PACK):
+            upper_part(0, t)
+        nc.vector.tensor_tensor(
+            w32_grouped[:, 1, :].rearrange("p (t m j) -> p m j t", t=PACK, j=PACK),
+            w2_raw[:].rearrange("p j (m t) -> p m j t", t=PACK),
+            sign[:].unsqueeze(1).unsqueeze(3).to_broadcast([P, P, PACK, PACK]),
+            ALU.mult,
+        )
+        w32_codes, w32_scales = quantize("w32", w32_grouped[:].rearrange("p u c -> p (u c)"), 1024)
+        w3_codes, w3_scales = w32_codes[:, 0:512], w32_scales[:, 0:512]
+        w2_codes, w2_scales = w32_codes[:, 512:1024], w32_scales[:, 512:1024]
+
+        h_win = [keep.tile([P, S], F32, name="h_win%d" % t) for t in range(PACK)]
+        h_acc = {}
+        for c, (lo, hi) in enumerate(CHUNKS):
+            w = hi - lo
+            upper = uppers[c]
+            lower = w2_raw[:, :, lo:hi]
+            for t in range(PACK):
+                if c > 0:
+                    upper_part(c, t)
+                for i in (1, 2):
+                    gather((c, t, i) in V_FIRST, got[c][i][:, t, :], y_win[t][:], first_lists[i][:, lo // 16 : hi // 16])
+                if t in LOWER_ENDS[c]:
+                    ts = slice(LOWER_ENDS[c][t], t + 1)
+                    nc.vector.tensor_tensor(lower[:, ts, :], got[c][1][:, ts, :], got[c][2][:, ts, :], ALU.max)
+            z = keep.tile([P, w * PACK], BF16, name="z%d" % c, align_bytes=64)
+            nc.vector.tensor_tensor(
+                z[:].rearrange("p (c i t) -> p c t i", i=4, t=PACK),
+                upper.rearrange("p t (c i) -> p c t i", i=4),
+                lower.rearrange("p t (c i) -> p c t i", i=4),
+                ALU.subtract,
+            )
+            z_codes, z_scales = quantize("z%d" % c, z[:], w)
+            for t in range(PACK):
+                tag = "bank%d" % (PACK * (1 - c) + t)
+                acc = psum.tile([P, S], F32, name="h" + tag, tag=tag)
+                cols = slice(t * P, (t + 1) * P)
+                nc.tensor.matmul_mx(out=acc[:, 0:w], lhsT=w3_codes[:, cols].bitcast(FP8X4), lhsT_scale=w3_scales[:, cols],
+                                    rhs=xb_words[:, lo:hi].bitcast(FP8X4), rhs_scale=xb_scales[:, lo:hi], start=True, stop=False)
+                h_acc[c, t] = acc
+            for t in range(PACK):
+                cols = slice(t * P, (t + 1) * P)
+                nc.tensor.matmul_mx(out=h_acc[c, t][:, 0:w], lhsT=w2_codes[:, cols].bitcast(FP8X4), lhsT_scale=w2_scales[:, cols],
+                                    rhs=z_codes[:].bitcast(FP8X4), rhs_scale=z_scales[:], start=False, stop=True)
+        for c, (lo, hi) in enumerate(CHUNKS):
+            for t in range(PACK):
+                nc.scalar.copy(h_win[t][:, lo:hi], h_acc[c, t][:, 0 : hi - lo])
+
+        out_view = out.rearrange("(p t) j -> p t j", t=PACK)
+        for t in range(PACK):
+            pair = [keep.tile([P, S], F32, name="pair%d_%d" % (t, i)) for i in range(2)]
+            top = keep.tile([P, S], F32, name="top%d" % t)
+            res = keep.tile([P, S], F32, name="res%d" % t)
+            pieces = CHUNKS if t == PACK - 1 else ((0, S),)
+            for lo, hi in pieces:
+                for i in range(2):
+                    for c, (a, b) in enumerate(CHUNKS):
+                        if lo <= a and b <= hi:
+                            gather((c, t, i) in V_SECOND, pair[i][:, a:b], h_win[t][:], second_lists[i][:, a // 16 : b // 16])
+                nc.vector.tensor_tensor(top[:, lo:hi], h_win[t][:, lo:hi], pair[0][:, lo:hi], ALU.max)
+                nc.vector.tensor_tensor(res[:, lo:hi], top[:, lo:hi], pair[1][:, lo:hi], ALU.min)
+                nc.sync.dma_start(out_view[:, t, lo:hi], res[:, lo:hi])

@@ -17,9 +17,9 @@ COPY = mybir.ActivationFunctionType.Copy
 
 P = 128
 PACK = 4
-CHUNKS = ((0, 256), (256, 512))
-LOWER_ENDS = ({3: 0}, {2: 0, 3: 3})
-V_FIRST = {(0, 0, 0), (0, 1, 0), (0, 2, 0), (0, 3, 0), (1, 0, 0)}
+CHUNKS = ((0, 256), (256, 384), (384, 512))
+HALVES = ((0, 256), (256, 512))
+LOWER_ENDS = ({3: 0}, {3: 0}, {2: 0, 3: 3})
 V_SECOND = {(0, 0, 0), (0, 0, 1), (1, 0, 0), (1, 0, 1), (0, 1, 0)}
 
 
@@ -48,7 +48,7 @@ def tile_picked_mixinmixminmx_none_p_kernel(
                 nc.scalar.activation(dst, window.indirect(offsets), COPY)
 
         def quantize(name, grouped, width):
-            codes = keep.tile([P, width], U32, name=name + "_codes", align_bytes=64)
+            codes = keep.tile([P, width], U32, name=name + "_codes", tag=name + "_codes", align_bytes=64)
             scales = keep.tile([P, width], U8, name=name + "_scales", align_bytes=64)
             nc.vector.quantize_mx(out=codes[:].bitcast(FP8X4), scales=scales[:], in_=grouped)
             return codes, scales
@@ -61,10 +61,11 @@ def tile_picked_mixinmixminmx_none_p_kernel(
         nc.sync.dma_start(gain[:], gn.rearrange("(p t) o -> p (t o)", t=PACK))
         w1_raw = load_weight("w1_raw", w1)
         for r in range(4):
-            nc.scalar.dma_start(x_bytes[r:P:32, :].bitcast(I32), x_scales[0, r:16:4, :].bitcast(I32))
+            nc.sync.dma_start(x_bytes[r:P:32, :].bitcast(I32), x_scales[0, r:16:4, :].bitcast(I32))
+        n1_t = load_list("n1_t", n1)
         x_tab = keep.tile([P, T], I32, name="x_tab")
         nc.sync.dma_start(x_tab[:], x_words[0].rearrange("p n r -> p (n r)").bitcast(I32))
-        first_lists = [load_list("n1_t", n1), load_list("n2_t", n2), load_list("n3_t", n3)]
+        first_lists = [n1_t, load_list("n2_t", n2), load_list("n3_t", n3)]
         w3_raw = load_weight("w3_raw", w3)
         w2_raw = load_weight("w2_raw", w2)
         second_lists = [load_list("n4_t", n4), load_list("n5_t", n5)]
@@ -87,10 +88,7 @@ def tile_picked_mixinmixminmx_none_p_kernel(
         for u in range(2):
             grouped = keep.tile([P, 2 * P * PACK], BF16, name="w1_grouped%d" % u, align_bytes=64)
             dst = grouped[:].rearrange("p (t m j) -> p m j t", t=2, j=PACK)
-            if u == 0:
-                nc.vector.tensor_copy(dst, w1_view[:, :, :, 0:2])
-            else:
-                nc.scalar.copy(dst, w1_view[:, :, :, 2:4])
+            nc.scalar.copy(dst, w1_view[:, :, :, 2 * u : 2 * u + 2])
             w1_grouped.append(grouped)
         for u in range(2):
             w1_q.append(quantize("w1_%d" % u, w1_grouped[u][:], 2 * P))
@@ -101,6 +99,7 @@ def tile_picked_mixinmixminmx_none_p_kernel(
         nc.vector.tensor_copy(xb_words[:], x_tab[:].bitcast(U32).indirect(two_t[:]))
 
         y_win = []
+        y_acc = []
         for t in range(PACK):
             acc = psum.tile([P, S], F32, name="bank%d" % t, tag="bank%d" % t)
             codes, scales = w1_q[t // 2]
@@ -110,47 +109,51 @@ def tile_picked_mixinmixminmx_none_p_kernel(
             win = keep.tile([P, S], F32, name="y_win%d" % t)
             nc.scalar.activation(win[:], acc[:], COPY, scale=size[:, t : t + 1])
             y_win.append(win)
+            y_acc.append(acc)
 
         w32_grouped = keep.tile([P, 2, 512 * PACK], BF16, name="w32_grouped", align_bytes=64)
-        nc.vector.tensor_copy(
-            w32_grouped[:, 0, :].rearrange("p (t m j) -> p m j t", t=PACK, j=PACK),
-            w3_raw[:].rearrange("p j (m t) -> p m j t", t=PACK),
+        nc.gpsimd.tensor_scalar(
+            w32_grouped[:, 0, :].rearrange("p (t m j) -> p m t j", t=PACK, j=PACK),
+            w3_raw[:].rearrange("p j (m t) -> p m t j", t=PACK),
+            1.0, 0.0, ALU.mult, ALU.add,
         )
-        got = [[keep.tile([P, PACK, hi - lo], F32, name="got%d_%d" % (c, i)) for i in range(3)] for c, (lo, hi) in enumerate(CHUNKS)]
-        upper0 = keep.tile([P, PACK, CHUNKS[0][1]], F32, name="upper0")
-        uppers = [upper0[:], w32_grouped[:, 0, :].bitcast(F32).rearrange("p (t w) -> p t w", t=PACK)]
-
-        def upper_part(c, t):
-            lo, hi = CHUNKS[c]
-            gather((c, t, 0) in V_FIRST, got[c][0][:, t, :], y_win[t][:], first_lists[0][:, lo // 16 : hi // 16])
-            nc.vector.tensor_tensor(uppers[c][:, t, :], y_win[t][:, lo:hi], got[c][0][:, t, :], ALU.max)
-
-        for t in range(PACK):
-            upper_part(0, t)
-        nc.vector.tensor_tensor(
-            w32_grouped[:, 1, :].rearrange("p (t m j) -> p m j t", t=PACK, j=PACK),
-            w2_raw[:].rearrange("p j (m t) -> p m j t", t=PACK),
-            sign[:].unsqueeze(1).unsqueeze(3).to_broadcast([P, P, PACK, PACK]),
+        nc.gpsimd.tensor_tensor(
+            w32_grouped[:, 1, :].rearrange("p (t m j) -> p m t j", t=PACK, j=PACK),
+            w2_raw[:].rearrange("p j (m t) -> p m t j", t=PACK),
+            sign[:].unsqueeze(1).unsqueeze(1).to_broadcast([P, P, PACK, PACK]),
             ALU.mult,
         )
+        far = keep.tile([P, 2, PACK, S], F32, name="far", tag="w1_1_codes", align_bytes=64)
+        near = keep.tile([P, PACK, S], F32, name="near")
+        upper_all = keep.tile([P, PACK, S], F32, name="upper_all")
+        for t in range(PACK):
+            for lo, hi in HALVES:
+                gather(True, near[:, t, lo:hi], y_win[t][:], first_lists[0][:, lo // 16 : hi // 16])
+            nc.vector.scalar_tensor_tensor(upper_all[:, t, :], y_acc[t][:], size[:, t : t + 1], near[:, t, :], ALU.mult, ALU.max)
         w32_codes, w32_scales = quantize("w32", w32_grouped[:].rearrange("p u c -> p (u c)"), 1024)
         w3_codes, w3_scales = w32_codes[:, 0:512], w32_scales[:, 0:512]
         w2_codes, w2_scales = w32_codes[:, 512:1024], w32_scales[:, 512:1024]
 
         h_win = [keep.tile([P, S], F32, name="h_win%d" % t) for t in range(PACK)]
         h_acc = {}
+        for u, (lo, hi) in enumerate(HALVES):
+            for t in range(PACK):
+                tag = "bank%d" % (PACK * (1 - u) + t)
+                acc = psum.tile([P, S], F32, name="h" + tag, tag=tag)
+                cols = slice(t * P, (t + 1) * P)
+                nc.tensor.matmul_mx(out=acc[:, 0 : hi - lo], lhsT=w3_codes[:, cols].bitcast(FP8X4), lhsT_scale=w3_scales[:, cols],
+                                    rhs=xb_words[:, lo:hi].bitcast(FP8X4), rhs_scale=xb_scales[:, lo:hi], start=True, stop=False)
+                h_acc[u, t] = acc
         for c, (lo, hi) in enumerate(CHUNKS):
             w = hi - lo
-            upper = uppers[c]
+            upper = upper_all[:, :, lo:hi]
             lower = w2_raw[:, :, lo:hi]
             for t in range(PACK):
-                if c > 0:
-                    upper_part(c, t)
-                for i in (1, 2):
-                    gather((c, t, i) in V_FIRST, got[c][i][:, t, :], y_win[t][:], first_lists[i][:, lo // 16 : hi // 16])
+                for i in range(2):
+                    gather(False, far[:, i, t, lo:hi], y_win[t][:], first_lists[1 + i][:, lo // 16 : hi // 16])
                 if t in LOWER_ENDS[c]:
                     ts = slice(LOWER_ENDS[c][t], t + 1)
-                    nc.vector.tensor_tensor(lower[:, ts, :], got[c][1][:, ts, :], got[c][2][:, ts, :], ALU.max)
+                    nc.vector.tensor_tensor(lower[:, ts, :], far[:, 0, ts, lo:hi], far[:, 1, ts, lo:hi], ALU.max)
             z = keep.tile([P, w * PACK], BF16, name="z%d" % c, align_bytes=64)
             nc.vector.tensor_tensor(
                 z[:].rearrange("p (c i t) -> p c t i", i=4, t=PACK),
@@ -159,30 +162,25 @@ def tile_picked_mixinmixminmx_none_p_kernel(
                 ALU.subtract,
             )
             z_codes, z_scales = quantize("z%d" % c, z[:], w)
-            for t in range(PACK):
-                tag = "bank%d" % (PACK * (1 - c) + t)
-                acc = psum.tile([P, S], F32, name="h" + tag, tag=tag)
-                cols = slice(t * P, (t + 1) * P)
-                nc.tensor.matmul_mx(out=acc[:, 0:w], lhsT=w3_codes[:, cols].bitcast(FP8X4), lhsT_scale=w3_scales[:, cols],
-                                    rhs=xb_words[:, lo:hi].bitcast(FP8X4), rhs_scale=xb_scales[:, lo:hi], start=True, stop=False)
-                h_acc[c, t] = acc
+            u = lo // 256
+            base = HALVES[u][0]
             for t in range(PACK):
                 cols = slice(t * P, (t + 1) * P)
-                nc.tensor.matmul_mx(out=h_acc[c, t][:, 0:w], lhsT=w2_codes[:, cols].bitcast(FP8X4), lhsT_scale=w2_scales[:, cols],
-                                    rhs=z_codes[:].bitcast(FP8X4), rhs_scale=z_scales[:], start=False, stop=True)
-        for c, (lo, hi) in enumerate(CHUNKS):
+                nc.tensor.matmul_mx(out=h_acc[u, t][:, lo - base : hi - base], lhsT=w2_codes[:, cols].bitcast(FP8X4), lhsT_scale=w2_scales[:, cols],
+                                    rhs=z_codes[:].bitcast(FP8X4), rhs_scale=z_scales[:], start=False, stop=(hi == HALVES[u][1]))
+        for u, (lo, hi) in enumerate(HALVES):
             for t in range(PACK):
-                nc.scalar.copy(h_win[t][:, lo:hi], h_acc[c, t][:, 0 : hi - lo])
+                nc.scalar.copy(h_win[t][:, lo:hi], h_acc[u, t][:, 0 : hi - lo])
 
         out_view = out.rearrange("(p t) j -> p t j", t=PACK)
         for t in range(PACK):
             pair = [keep.tile([P, S], F32, name="pair%d_%d" % (t, i)) for i in range(2)]
             top = keep.tile([P, S], F32, name="top%d" % t)
             res = keep.tile([P, S], F32, name="res%d" % t)
-            pieces = CHUNKS if t == PACK - 1 else ((0, S),)
+            pieces = HALVES if t == PACK - 1 else ((0, S),)
             for lo, hi in pieces:
                 for i in range(2):
-                    for c, (a, b) in enumerate(CHUNKS):
+                    for c, (a, b) in enumerate(HALVES):
                         if lo <= a and b <= hi:
                             gather((c, t, i) in V_SECOND, pair[i][:, a:b], h_win[t][:], second_lists[i][:, a // 16 : b // 16])
                 nc.vector.tensor_tensor(top[:, lo:hi], h_win[t][:, lo:hi], pair[0][:, lo:hi], ALU.max)

@@ -19,7 +19,6 @@ P = 128
 PACK = 4
 CHUNKS = ((0, 256), (256, 384), (384, 512))
 HALVES = ((0, 256), (256, 512))
-LOWER_ENDS = ({3: 0}, {3: 0}, {2: 0, 3: 3})
 V_SECOND = {(0, 0, 0), (0, 0, 1), (1, 0, 0), (1, 0, 1), (0, 1, 0)}
 
 
@@ -59,21 +58,20 @@ def tile_picked_mixinmixminmx_none_p_kernel(
         two_t = load_list("two_t", two)
         gain = keep.tile([P, PACK], F32, name="gain")
         nc.sync.dma_start(gain[:], gn.rearrange("(p t) o -> p (t o)", t=PACK))
-        w1_raw = load_weight("w1_raw", w1)
-        for r in range(4):
-            nc.sync.dma_start(x_bytes[r:P:32, :].bitcast(I32), x_scales[0, r:16:4, :].bitcast(I32))
-        n1_t = load_list("n1_t", n1)
         x_tab = keep.tile([P, T], I32, name="x_tab")
         nc.sync.dma_start(x_tab[:], x_words[0].rearrange("p n r -> p (n r)").bitcast(I32))
-        first_lists = [n1_t, load_list("n2_t", n2), load_list("n3_t", n3)]
+        for r in range(4):
+            nc.sync.dma_start(x_bytes[r:P:32, :].bitcast(I32), x_scales[0, r:16:4, :].bitcast(I32))
+        w1_rows = w1.rearrange("(p j) c -> p j c", j=PACK)
+        w1_raw = []
+        for v, (lo, hi) in enumerate(HALVES):
+            part = keep.tile([P, PACK, hi - lo], F32, name="w1_raw%d" % v, tag="raw%d" % v, align_bytes=64)
+            nc.sync.dma_start(part[:], w1_rows[:, :, lo:hi])
+            w1_raw.append(part)
+        first_lists = [load_list("n1_t", n1), load_list("n2_t", n2), load_list("n3_t", n3)]
         w3_raw = load_weight("w3_raw", w3)
         w2_raw = load_weight("w2_raw", w2)
         second_lists = [load_list("n4_t", n4), load_list("n5_t", n5)]
-
-        xa_scales = keep.tile([P, S], U8, name="xa_scales", align_bytes=64)
-        nc.vector.tensor_copy(xa_scales[:], x_bytes[:].indirect(offs_t[:]))
-        xb_scales = keep.tile([P, S], U8, name="xb_scales", align_bytes=64)
-        nc.vector.tensor_copy(xb_scales[:], x_bytes[:].indirect(two_t[:]))
 
         half = keep.tile([P, PACK], F32, name="half")
         nc.vector.tensor_scalar(half[:], gain[:], 0.0, 2.0, ALU.is_ge, ALU.mult)
@@ -82,21 +80,24 @@ def tile_picked_mixinmixminmx_none_p_kernel(
         size = keep.tile([P, PACK], F32, name="size")
         nc.vector.tensor_tensor(size[:], gain[:], sign[:], ALU.mult)
 
-        w1_q = []
-        w1_view = w1_raw[:].rearrange("p j (m t) -> p m j t", t=PACK)
-        w1_grouped = []
-        for u in range(2):
-            grouped = keep.tile([P, 2 * P * PACK], BF16, name="w1_grouped%d" % u, align_bytes=64)
-            dst = grouped[:].rearrange("p (t m j) -> p m j t", t=2, j=PACK)
-            nc.scalar.copy(dst, w1_view[:, :, :, 2 * u : 2 * u + 2])
-            w1_grouped.append(grouped)
-        for u in range(2):
-            w1_q.append(quantize("w1_%d" % u, w1_grouped[u][:], 2 * P))
-
         xa_words = keep.tile([P, S], U32, name="xa_words", align_bytes=64)
         nc.vector.tensor_copy(xa_words[:], x_tab[:].bitcast(U32).indirect(offs_t[:]))
+        xa_scales = keep.tile([P, S], U8, name="xa_scales", align_bytes=64)
+        nc.vector.tensor_copy(xa_scales[:], x_bytes[:].indirect(offs_t[:]))
         xb_words = keep.tile([P, S], U32, name="xb_words", align_bytes=64)
         nc.vector.tensor_copy(xb_words[:], x_tab[:].bitcast(U32).indirect(two_t[:]))
+
+        w1_grouped = [
+            keep.tile([P, 2 * P * PACK], BF16, name="w1_grouped%d" % u, tag="stage%d" % u, align_bytes=64) for u in range(2)
+        ]
+        for v in range(2):
+            for u in range(2):
+                dst = w1_grouped[u][:].rearrange("p (t m j) -> p m j t", t=2, j=PACK)
+                src = w1_raw[v][:].rearrange("p j (m t) -> p m j t", t=PACK)
+                nc.scalar.copy(dst[:, 64 * v : 64 * (v + 1), :, :], src[:, :, :, 2 * u : 2 * u + 2])
+        w1_q = [quantize("w1_%d" % u, w1_grouped[u][:], 2 * P) for u in range(2)]
+        xb_scales = keep.tile([P, S], U8, name="xb_scales", tag="raw1", align_bytes=64)
+        nc.vector.tensor_copy(xb_scales[:], x_bytes[:].indirect(two_t[:]))
 
         y_win = []
         y_acc = []
@@ -111,7 +112,7 @@ def tile_picked_mixinmixminmx_none_p_kernel(
             y_win.append(win)
             y_acc.append(acc)
 
-        w32_grouped = keep.tile([P, 2, 512 * PACK], BF16, name="w32_grouped", align_bytes=64)
+        w32_grouped = keep.tile([P, 2, 512 * PACK], BF16, name="w32_grouped", tag="stage1", align_bytes=64)
         nc.gpsimd.tensor_scalar(
             w32_grouped[:, 0, :].rearrange("p (t m j) -> p m t j", t=PACK, j=PACK),
             w3_raw[:].rearrange("p j (m t) -> p m t j", t=PACK),
@@ -129,60 +130,78 @@ def tile_picked_mixinmixminmx_none_p_kernel(
         for t in range(PACK):
             for lo, hi in HALVES:
                 gather(True, near[:, t, lo:hi], y_win[t][:], first_lists[0][:, lo // 16 : hi // 16])
-            nc.vector.scalar_tensor_tensor(upper_all[:, t, :], y_acc[t][:], size[:, t : t + 1], near[:, t, :], ALU.mult, ALU.max)
+            for lo, hi in HALVES:
+                nc.vector.scalar_tensor_tensor(
+                    upper_all[:, t, lo:hi], y_acc[t][:, lo:hi], size[:, t : t + 1], near[:, t, lo:hi], ALU.mult, ALU.max
+                )
         w32_codes, w32_scales = quantize("w32", w32_grouped[:].rearrange("p u c -> p (u c)"), 1024)
         w3_codes, w3_scales = w32_codes[:, 0:512], w32_scales[:, 0:512]
         w2_codes, w2_scales = w32_codes[:, 512:1024], w32_scales[:, 512:1024]
 
         h_win = [keep.tile([P, S], F32, name="h_win%d" % t) for t in range(PACK)]
         h_acc = {}
-        for u, (lo, hi) in enumerate(HALVES):
+
+        def open_chunk(c):
+            lo, hi = CHUNKS[c]
             for t in range(PACK):
-                tag = "bank%d" % (PACK * (1 - u) + t)
-                acc = psum.tile([P, S], F32, name="h" + tag, tag=tag)
+                tag = "bank%d" % (PACK * ((c + 1) % 2) + t)
+                acc = psum.tile([P, S], F32, name="h%d_%d" % (c, t), tag=tag)
                 cols = slice(t * P, (t + 1) * P)
                 nc.tensor.matmul_mx(out=acc[:, 0 : hi - lo], lhsT=w3_codes[:, cols].bitcast(FP8X4), lhsT_scale=w3_scales[:, cols],
                                     rhs=xb_words[:, lo:hi].bitcast(FP8X4), rhs_scale=xb_scales[:, lo:hi], start=True, stop=False)
-                h_acc[u, t] = acc
+                h_acc[c, t] = acc
+
+        def empty_chunk(c):
+            lo, hi = CHUNKS[c]
+            for t in range(PACK):
+                if c == len(CHUNKS) - 1 and t == 0:
+                    nc.vector.tensor_copy(h_win[t][:, lo:hi], h_acc[c, t][:, 0 : hi - lo])
+                else:
+                    nc.scalar.copy(h_win[t][:, lo:hi], h_acc[c, t][:, 0 : hi - lo])
+
+        z_q = []
         for c, (lo, hi) in enumerate(CHUNKS):
             w = hi - lo
-            upper = upper_all[:, :, lo:hi]
-            lower = w2_raw[:, :, lo:hi]
+            last = c == len(CHUNKS) - 1
             for t in range(PACK):
                 for i in range(2):
                     gather(False, far[:, i, t, lo:hi], y_win[t][:], first_lists[1 + i][:, lo // 16 : hi // 16])
-                if t in LOWER_ENDS[c]:
-                    ts = slice(LOWER_ENDS[c][t], t + 1)
-                    nc.vector.tensor_tensor(lower[:, ts, :], far[:, 0, ts, lo:hi], far[:, 1, ts, lo:hi], ALU.max)
-            z = keep.tile([P, w * PACK], BF16, name="z%d" % c, align_bytes=64)
-            nc.vector.tensor_tensor(
-                z[:].rearrange("p (c i t) -> p c t i", i=4, t=PACK),
-                upper.rearrange("p t (c i) -> p c t i", i=4),
-                lower.rearrange("p t (c i) -> p c t i", i=4),
-                ALU.subtract,
-            )
-            z_codes, z_scales = quantize("z%d" % c, z[:], w)
-            u = lo // 256
-            base = HALVES[u][0]
+            z_codes = keep.tile([P, w], U32, name="z_codes%d" % c, align_bytes=64)
+            z_scales = keep.tile([P, w], U8, name="z_scales%d" % c, align_bytes=64)
+            for a in range(lo, hi, 128):
+                cols = slice(a, a + 128)
+                for ts in (slice(0, 3), slice(3, 4)) if last else (slice(0, 4),):
+                    nc.vector.tensor_tensor(w2_raw[:, ts, cols], far[:, 0, ts, cols], far[:, 1, ts, cols], ALU.max)
+                z = keep.tile([P, 128 * PACK], BF16, name="z%d" % a, align_bytes=64)
+                nc.vector.tensor_tensor(
+                    z[:].rearrange("p (c i t) -> p c t i", i=2, t=PACK),
+                    upper_all[:, :, cols].rearrange("p t (c i) -> p c t i", i=2),
+                    w2_raw[:, :, cols].rearrange("p t (c i) -> p c t i", i=2),
+                    ALU.subtract,
+                )
+                part = slice(a - lo, a - lo + 128)
+                nc.vector.quantize_mx(out=z_codes[:, part].bitcast(FP8X4), scales=z_scales[:, part], in_=z[:])
+            z_q.append((z_codes, z_scales))
+        for c, (lo, hi) in enumerate(CHUNKS):
+            open_chunk(c)
+            z_codes, z_scales = z_q[c]
             for t in range(PACK):
                 cols = slice(t * P, (t + 1) * P)
-                nc.tensor.matmul_mx(out=h_acc[u, t][:, lo - base : hi - base], lhsT=w2_codes[:, cols].bitcast(FP8X4), lhsT_scale=w2_scales[:, cols],
-                                    rhs=z_codes[:].bitcast(FP8X4), rhs_scale=z_scales[:], start=False, stop=(hi == HALVES[u][1]))
-        for u, (lo, hi) in enumerate(HALVES):
-            for t in range(PACK):
-                nc.scalar.copy(h_win[t][:, lo:hi], h_acc[u, t][:, 0 : hi - lo])
+                nc.tensor.matmul_mx(out=h_acc[c, t][:, 0 : hi - lo], lhsT=w2_codes[:, cols].bitcast(FP8X4), lhsT_scale=w2_scales[:, cols],
+                                    rhs=z_codes[:].bitcast(FP8X4), rhs_scale=z_scales[:], start=False, stop=True)
+            empty_chunk(c)
 
         out_view = out.rearrange("(p t) j -> p t j", t=PACK)
         for t in range(PACK):
             pair = [keep.tile([P, S], F32, name="pair%d_%d" % (t, i)) for i in range(2)]
             top = keep.tile([P, S], F32, name="top%d" % t)
             res = keep.tile([P, S], F32, name="res%d" % t)
-            pieces = HALVES if t == PACK - 1 else ((0, S),)
-            for lo, hi in pieces:
-                for i in range(2):
-                    for c, (a, b) in enumerate(HALVES):
-                        if lo <= a and b <= hi:
-                            gather((c, t, i) in V_SECOND, pair[i][:, a:b], h_win[t][:], second_lists[i][:, a // 16 : b // 16])
-                nc.vector.tensor_tensor(top[:, lo:hi], h_win[t][:, lo:hi], pair[0][:, lo:hi], ALU.max)
+            last = t == PACK - 1
+            for c, (a, b) in enumerate(HALVES):
+                gather((c, t, 0) in V_SECOND, pair[0][:, a:b], h_win[t][:], second_lists[0][:, a // 16 : b // 16])
+            nc.vector.tensor_tensor(top[:], h_win[t][:], pair[0][:], ALU.max)
+            for c, (a, b) in enumerate(CHUNKS if last else HALVES):
+                gather((c, t, 1) in V_SECOND, pair[1][:, a:b], h_win[t][:], second_lists[1][:, a // 16 : b // 16])
+            for lo, hi in CHUNKS if last else ((0, S),):
                 nc.vector.tensor_tensor(res[:, lo:hi], top[:, lo:hi], pair[1][:, lo:hi], ALU.min)
                 nc.sync.dma_start(out_view[:, t, lo:hi], res[:, lo:hi])

@@ -56,10 +56,10 @@ def tile_picked_mixinmixminmx_none_p_kernel(
         nc.vector.memset(x_bytes[:].bitcast(I32), 0)
         offs_t = load_list("offs_t", offs)
         two_t = load_list("two_t", two)
-        gain = keep.tile([P, PACK], F32, name="gain")
-        nc.sync.dma_start(gain[:], gn.rearrange("(p t) o -> p (t o)", t=PACK))
         x_tab = keep.tile([P, T], I32, name="x_tab")
         nc.sync.dma_start(x_tab[:], x_words[0].rearrange("p n r -> p (n r)").bitcast(I32))
+        gain = keep.tile([P, PACK], F32, name="gain")
+        nc.sync.dma_start(gain[:], gn.rearrange("(p t) o -> p (t o)", t=PACK))
         for r in range(4):
             nc.sync.dma_start(x_bytes[r:P:32, :].bitcast(I32), x_scales[0, r:16:4, :].bitcast(I32))
         w1_rows = w1.rearrange("(p j) c -> p j c", j=PACK)
@@ -73,12 +73,12 @@ def tile_picked_mixinmixminmx_none_p_kernel(
         w2_raw = load_weight("w2_raw", w2)
         second_lists = [load_list("n4_t", n4), load_list("n5_t", n5)]
 
-        half = keep.tile([P, PACK], F32, name="half")
-        nc.vector.tensor_scalar(half[:], gain[:], 0.0, 2.0, ALU.is_ge, ALU.mult)
-        sign = keep.tile([P, PACK], F32, name="sign")
-        nc.vector.tensor_scalar(sign[:], half[:], -1.0, None, ALU.add)
         size = keep.tile([P, PACK], F32, name="size")
-        nc.vector.tensor_tensor(size[:], gain[:], sign[:], ALU.mult)
+        nc.scalar.activation(size[:], gain[:], mybir.ActivationFunctionType.Abs)
+        half = keep.tile([P, PACK], F32, name="half")
+        nc.gpsimd.tensor_scalar(half[:], gain[:], 0.0, 2.0, ALU.is_ge, ALU.mult)
+        sign = keep.tile([P, PACK], F32, name="sign")
+        nc.gpsimd.tensor_scalar(sign[:], half[:], 1.0, -1.0, ALU.mult, ALU.add)
 
         xa_words = keep.tile([P, S], U32, name="xa_words", align_bytes=64)
         nc.vector.tensor_copy(xa_words[:], x_tab[:].bitcast(U32).indirect(offs_t[:]))
@@ -100,17 +100,20 @@ def tile_picked_mixinmixminmx_none_p_kernel(
         nc.vector.tensor_copy(xb_scales[:], x_bytes[:].indirect(two_t[:]))
 
         y_win = []
-        y_acc = []
+        y_acc = {}
         for t in range(PACK):
-            acc = psum.tile([P, S], F32, name="bank%d" % t, tag="bank%d" % t)
             codes, scales = w1_q[t // 2]
             cols = slice((t % 2) * P, (t % 2 + 1) * P)
-            nc.tensor.matmul_mx(out=acc[:], lhsT=codes[:, cols].bitcast(FP8X4), lhsT_scale=scales[:, cols],
-                                rhs=xa_words[:].bitcast(FP8X4), rhs_scale=xa_scales[:], start=True, stop=True)
             win = keep.tile([P, S], F32, name="y_win%d" % t)
-            nc.scalar.activation(win[:], acc[:], COPY, scale=size[:, t : t + 1])
+            for u, (lo, hi) in enumerate(HALVES if t == 0 else ((0, S),)):
+                acc = psum.tile([P, S], F32, name="y%d_%d" % (t, u), tag="bank%d" % (PACK * u + t))
+                nc.tensor.matmul_mx(out=acc[:, 0 : hi - lo], lhsT=codes[:, cols].bitcast(FP8X4), lhsT_scale=scales[:, cols],
+                                    rhs=xa_words[:, lo:hi].bitcast(FP8X4), rhs_scale=xa_scales[:, lo:hi], start=True, stop=True)
+                nc.scalar.activation(win[:, lo:hi], acc[:, 0 : hi - lo], COPY, scale=size[:, t : t + 1])
+                for a, b in HALVES:
+                    if lo <= a and b <= hi:
+                        y_acc[t, a] = acc[:, a - lo : b - lo]
             y_win.append(win)
-            y_acc.append(acc)
 
         w32_grouped = keep.tile([P, 2, 512 * PACK], BF16, name="w32_grouped", tag="stage1", align_bytes=64)
         nc.gpsimd.tensor_scalar(
@@ -132,7 +135,7 @@ def tile_picked_mixinmixminmx_none_p_kernel(
                 gather(True, near[:, t, lo:hi], y_win[t][:], first_lists[0][:, lo // 16 : hi // 16])
             for lo, hi in HALVES:
                 nc.vector.scalar_tensor_tensor(
-                    upper_all[:, t, lo:hi], y_acc[t][:, lo:hi], size[:, t : t + 1], near[:, t, lo:hi], ALU.mult, ALU.max
+                    upper_all[:, t, lo:hi], y_acc[t, lo], size[:, t : t + 1], near[:, t, lo:hi], ALU.mult, ALU.max
                 )
         w32_codes, w32_scales = quantize("w32", w32_grouped[:].rearrange("p u c -> p (u c)"), 1024)
         w3_codes, w3_scales = w32_codes[:, 0:512], w32_scales[:, 0:512]

@@ -69,8 +69,13 @@ def tile_picked_mixinmixminmx_none_p_kernel(
             nc.sync.dma_start(part[:], w1_rows[:, :, lo:hi])
             w1_raw.append(part)
         first_lists = [load_list("n1_t", n1), load_list("n2_t", n2), load_list("n3_t", n3)]
+        w2_rows = w2.rearrange("(p j) c -> p j c", j=PACK)
+        w2_raw = []
+        for v, (lo, hi) in enumerate(HALVES):
+            part = keep.tile([P, PACK, hi - lo], F32, name="w2_raw%d" % v)
+            nc.sync.dma_start(part[:], w2_rows[:, :, lo:hi])
+            w2_raw.append(part)
         w3_raw = load_weight("w3_raw", w3)
-        w2_raw = load_weight("w2_raw", w2)
         second_lists = [load_list("n4_t", n4), load_list("n5_t", n5)]
 
         size = keep.tile([P, PACK], F32, name="size")
@@ -116,16 +121,18 @@ def tile_picked_mixinmixminmx_none_p_kernel(
             y_win.append(win)
 
         w32_grouped = keep.tile([P, 2, 512 * PACK], BF16, name="w32_grouped", tag="stage1", align_bytes=64)
+        w2_dst = w32_grouped[:, 0, :].rearrange("p (t m j) -> p m t j", t=PACK, j=PACK)
+        for v in range(2):
+            nc.gpsimd.tensor_tensor(
+                w2_dst[:, 64 * v : 64 * (v + 1), :, :],
+                w2_raw[v][:].rearrange("p j (m t) -> p m t j", t=PACK),
+                sign[:].unsqueeze(1).unsqueeze(1).to_broadcast([P, 64, PACK, PACK]),
+                ALU.mult,
+            )
         nc.gpsimd.tensor_scalar(
-            w32_grouped[:, 0, :].rearrange("p (t m j) -> p m t j", t=PACK, j=PACK),
+            w32_grouped[:, 1, :].rearrange("p (t m j) -> p m t j", t=PACK, j=PACK),
             w3_raw[:].rearrange("p j (m t) -> p m t j", t=PACK),
             1.0, 0.0, ALU.mult, ALU.add,
-        )
-        nc.gpsimd.tensor_tensor(
-            w32_grouped[:, 1, :].rearrange("p (t m j) -> p m t j", t=PACK, j=PACK),
-            w2_raw[:].rearrange("p j (m t) -> p m t j", t=PACK),
-            sign[:].unsqueeze(1).unsqueeze(1).to_broadcast([P, P, PACK, PACK]),
-            ALU.mult,
         )
         far = keep.tile([P, 2, PACK, S], F32, name="far", tag="w1_1_codes", align_bytes=64)
         near = keep.tile([P, PACK, S], F32, name="near")
@@ -138,8 +145,8 @@ def tile_picked_mixinmixminmx_none_p_kernel(
                     upper_all[:, t, lo:hi], y_acc[t, lo], size[:, t : t + 1], near[:, t, lo:hi], ALU.mult, ALU.max
                 )
         w32_codes, w32_scales = quantize("w32", w32_grouped[:].rearrange("p u c -> p (u c)"), 1024)
-        w3_codes, w3_scales = w32_codes[:, 0:512], w32_scales[:, 0:512]
-        w2_codes, w2_scales = w32_codes[:, 512:1024], w32_scales[:, 512:1024]
+        w2_codes, w2_scales = w32_codes[:, 0:512], w32_scales[:, 0:512]
+        w3_codes, w3_scales = w32_codes[:, 512:1024], w32_scales[:, 512:1024]
 
         h_win = [keep.tile([P, S], F32, name="h_win%d" % t) for t in range(PACK)]
         h_acc = {}
@@ -174,12 +181,12 @@ def tile_picked_mixinmixminmx_none_p_kernel(
             for a in range(lo, hi, 128):
                 cols = slice(a, a + 128)
                 for ts in (slice(0, 3), slice(3, 4)) if last else (slice(0, 4),):
-                    nc.vector.tensor_tensor(w2_raw[:, ts, cols], far[:, 0, ts, cols], far[:, 1, ts, cols], ALU.max)
+                    nc.vector.tensor_tensor(w3_raw[:, ts, cols], far[:, 0, ts, cols], far[:, 1, ts, cols], ALU.max)
                 z = keep.tile([P, 128 * PACK], BF16, name="z%d" % a, align_bytes=64)
                 nc.vector.tensor_tensor(
                     z[:].rearrange("p (c i t) -> p c t i", i=2, t=PACK),
                     upper_all[:, :, cols].rearrange("p t (c i) -> p c t i", i=2),
-                    w2_raw[:, :, cols].rearrange("p t (c i) -> p c t i", i=2),
+                    w3_raw[:, :, cols].rearrange("p t (c i) -> p c t i", i=2),
                     ALU.subtract,
                 )
                 part = slice(a - lo, a - lo + 128)

from contextlib import ExitStack

import concourse.mybir as mybir

K, T, S, H, N = 512, 2048, 512, 512, 512
FLOPS = 2 * S * (K * H + H * N + K * N)

F32 = mybir.dt.float32
BF16 = mybir.dt.bfloat16
I32 = mybir.dt.int32
U32 = mybir.dt.uint32
U16 = mybir.dt.uint16
U8 = mybir.dt.uint8
FP8X4 = mybir.dt.float8_e4m3fn_x4
ALU = mybir.AluOpType
COPY = mybir.ActivationFunctionType.Copy

P = 128
PACK = 4
CHUNKS = ((0, 256), (256, 384), (384, 512))
HALVES = ((0, 256), (256, 512))
V_SECOND = {(0, 0, 0), (0, 0, 1), (1, 0, 0), (1, 0, 1), (0, 1, 0)}


def tile_picked_mixinmixminmx_none_p_kernel(
    tc, x_words, x_scales, w1, gn, w2, w3, offs, n1, n2, n3, two, n4, n5, out
):
    nc = tc.nc
    with ExitStack() as ctx:
        keep = ctx.enter_context(tc.tile_pool(name="keep", bufs=1))
        psum = ctx.enter_context(tc.psum_pool(name="psum", bufs=1))

        def load_list(name, src):
            tile = keep.tile([P, S // 16], U16, name=name)
            nc.sync.dma_start(tile[:], src)
            return tile

        def load_weight(name, src):
            tile = keep.tile([P, PACK, 512], F32, name=name)
            nc.sync.dma_start(tile[:], src.rearrange("(p j) c -> p j c", j=PACK))
            return tile

        def gather(on_vector, dst, window, offsets):
            if on_vector:
                nc.vector.tensor_copy(dst, window.indirect(offsets))
            else:
                nc.scalar.activation(dst, window.indirect(offsets), COPY)

        def quantize(name, grouped, width):
            codes = keep.tile([P, width], U32, name=name + "_codes", tag=name + "_codes", align_bytes=64)
            scales = keep.tile([P, width], U8, name=name + "_scales", align_bytes=64)
            nc.vector.quantize_mx(out=codes[:].bitcast(FP8X4), scales=scales[:], in_=grouped)
            return codes, scales

        x_bytes = keep.tile([P, T], U8, name="x_bytes")
        nc.vector.memset(x_bytes[:].bitcast(I32), 0)
        offs_t = load_list("offs_t", offs)
        two_t = load_list("two_t", two)
        x_tab = keep.tile([P, T], I32, name="x_tab")
        nc.sync.dma_start(x_tab[:], x_words[0].rearrange("p n r -> p (n r)").bitcast(I32))
        gain = keep.tile([P, PACK], F32, name="gain")
        nc.sync.dma_start(gain[:], gn.rearrange("(p t) o -> p (t o)", t=PACK))
        for r in range(4):
            nc.sync.dma_start(x_bytes[r:P:32, :].bitcast(I32), x_scales[0, r:16:4, :].bitcast(I32))
        w1_rows = w1.rearrange("(p j) c -> p j c", j=PACK)
        w1_raw = []
        for v, (lo, hi) in enumerate(HALVES):
            part = keep.tile([P, PACK, hi - lo], F32, name="w1_raw%d" % v, tag="raw%d" % v, align_bytes=64)
            nc.sync.dma_start(part[:], w1_rows[:, :, lo:hi])
            w1_raw.append(part)
        first_lists = [load_list("n1_t", n1), load_list("n2_t", n2), load_list("n3_t", n3)]
        w2_rows = w2.rearrange("(p j) c -> p j c", j=PACK)
        w2_raw = []
        for v, (lo, hi) in enumerate(HALVES):
            part = keep.tile([P, PACK, hi - lo], F32, name="w2_raw%d" % v)
            nc.sync.dma_start(part[:], w2_rows[:, :, lo:hi])
            w2_raw.append(part)
        w3_raw = load_weight("w3_raw", w3)
        second_lists = [load_list("n4_t", n4), load_list("n5_t", n5)]

        size = keep.tile([P, PACK], F32, name="size")
        nc.scalar.activation(size[:], gain[:], mybir.ActivationFunctionType.Abs)
        half = keep.tile([P, PACK], F32, name="half")
        nc.gpsimd.tensor_scalar(half[:], gain[:], 0.0, 2.0, ALU.is_ge, ALU.mult)
        sign = keep.tile([P, PACK], F32, name="sign")
        nc.gpsimd.tensor_scalar(sign[:], half[:], 1.0, -1.0, ALU.mult, ALU.add)

        xa_words = keep.tile([P, S], U32, name="xa_words", align_bytes=64)
        nc.vector.tensor_copy(xa_words[:], x_tab[:].bitcast(U32).indirect(offs_t[:]))
        xa_scales = keep.tile([P, S], U8, name="xa_scales", align_bytes=64)
        nc.vector.tensor_copy(xa_scales[:], x_bytes[:].indirect(offs_t[:]))
        xb_words = keep.tile([P, S], U32, name="xb_words", align_bytes=64)
        nc.vector.tensor_copy(xb_words[:], x_tab[:].bitcast(U32).indirect(two_t[:]))

        w1_grouped = [
            keep.tile([P, 2 * P * PACK], BF16, name="w1_grouped%d" % u, tag="stage%d" % u, align_bytes=64) for u in range(2)
        ]
        for v in range(2):
            for u in range(2):
                dst = w1_grouped[u][:].rearrange("p (t m j) -> p m j t", t=2, j=PACK)
                src = w1_raw[v][:].rearrange("p j (m t) -> p m j t", t=PACK)
                nc.scalar.copy(dst[:, 64 * v : 64 * (v + 1), :, :], src[:, :, :, 2 * u : 2 * u + 2])
        w1_q = [quantize("w1_%d" % u, w1_grouped[u][:], 2 * P) for u in range(2)]
        xb_scales = keep.tile([P, S], U8, name="xb_scales", tag="raw1", align_bytes=64)
        nc.vector.tensor_copy(xb_scales[:], x_bytes[:].indirect(two_t[:]))

        y_win = []
        y_acc = {}
        for t in range(PACK):
            codes, scales = w1_q[t // 2]
            cols = slice((t % 2) * P, (t % 2 + 1) * P)
            win = keep.tile([P, S], F32, name="y_win%d" % t)
            for u, (lo, hi) in enumerate(HALVES if t == 0 else ((0, S),)):
                acc = psum.tile([P, S], F32, name="y%d_%d" % (t, u), tag="bank%d" % (PACK * u + t))
                nc.tensor.matmul_mx(out=acc[:, 0 : hi - lo], lhsT=codes[:, cols].bitcast(FP8X4), lhsT_scale=scales[:, cols],
                                    rhs=xa_words[:, lo:hi].bitcast(FP8X4), rhs_scale=xa_scales[:, lo:hi], start=True, stop=True)
                nc.scalar.activation(win[:, lo:hi], acc[:, 0 : hi - lo], COPY, scale=size[:, t : t + 1])
                for a, b in HALVES:
                    if lo <= a and b <= hi:
                        y_acc[t, a] = acc[:, a - lo : b - lo]
            y_win.append(win)

        w32_grouped = keep.tile([P, 2, 512 * PACK], BF16, name="w32_grouped", tag="stage1", align_bytes=64)
        w2_dst = w32_grouped[:, 0, :].rearrange("p (t m j) -> p m t j", t=PACK, j=PACK)
        for v in range(2):
            nc.gpsimd.tensor_tensor(
                w2_dst[:, 64 * v : 64 * (v + 1), :, :],
                w2_raw[v][:].rearrange("p j (m t) -> p m t j", t=PACK),
                sign[:].unsqueeze(1).unsqueeze(1).to_broadcast([P, 64, PACK, PACK]),
                ALU.mult,
            )
        nc.gpsimd.tensor_scalar(
            w32_grouped[:, 1, :].rearrange("p (t m j) -> p m t j", t=PACK, j=PACK),
            w3_raw[:].rearrange("p j (m t) -> p m t j", t=PACK),
            1.0, 0.0, ALU.mult, ALU.add,
        )
        far = keep.tile([P, 2, PACK, S], F32, name="far", tag="w1_1_codes", align_bytes=64)
        near = keep.tile([P, PACK, S], F32, name="near")
        upper_all = keep.tile([P, PACK, S], F32, name="upper_all")
        for t in range(PACK):
            for lo, hi in HALVES:
                gather(True, near[:, t, lo:hi], y_win[t][:], first_lists[0][:, lo // 16 : hi // 16])
            for lo, hi in HALVES:
                nc.vector.scalar_tensor_tensor(
                    upper_all[:, t, lo:hi], y_acc[t, lo], size[:, t : t + 1], near[:, t, lo:hi], ALU.mult, ALU.max
                )
        w32_codes, w32_scales = quantize("w32", w32_grouped[:].rearrange("p u c -> p (u c)"), 1024)
        w2_codes, w2_scales = w32_codes[:, 0:512], w32_scales[:, 0:512]
        w3_codes, w3_scales = w32_codes[:, 512:1024], w32_scales[:, 512:1024]

        h_win = [keep.tile([P, S], F32, name="h_win%d" % t) for t in range(PACK)]
        h_acc = {}

        def open_chunk(c):
            lo, hi = CHUNKS[c]
            for t in range(PACK):
                tag = "bank%d" % (PACK * ((c + 1) % 2) + t)
                acc = psum.tile([P, S], F32, name="h%d_%d" % (c, t), tag=tag)
                cols = slice(t * P, (t + 1) * P)
                nc.tensor.matmul_mx(out=acc[:, 0 : hi - lo], lhsT=w3_codes[:, cols].bitcast(FP8X4), lhsT_scale=w3_scales[:, cols],
                                    rhs=xb_words[:, lo:hi].bitcast(FP8X4), rhs_scale=xb_scales[:, lo:hi], start=True, stop=False)
                h_acc[c, t] = acc

        def empty_chunk(c):
            lo, hi = CHUNKS[c]
            for t in range(PACK):
                if c == len(CHUNKS) - 1 and t == 0:
                    nc.vector.tensor_copy(h_win[t][:, lo:hi], h_acc[c, t][:, 0 : hi - lo])
                else:
                    nc.scalar.copy(h_win[t][:, lo:hi], h_acc[c, t][:, 0 : hi - lo])

        z_q = []
        for c, (lo, hi) in enumerate(CHUNKS):
            w = hi - lo
            last = c == len(CHUNKS) - 1
            for t in range(PACK):
                for i in range(2):
                    gather(False, far[:, i, t, lo:hi], y_win[t][:], first_lists[1 + i][:, lo // 16 : hi // 16])
            z_codes = keep.tile([P, w], U32, name="z_codes%d" % c, align_bytes=64)
            z_scales = keep.tile([P, w], U8, name="z_scales%d" % c, align_bytes=64)
            for a in range(lo, hi, 128):
                cols = slice(a, a + 128)
                for ts in (slice(0, 3), slice(3, 4)) if last else (slice(0, 4),):
                    nc.vector.tensor_tensor(w3_raw[:, ts, cols], far[:, 0, ts, cols], far[:, 1, ts, cols], ALU.max)
                z = keep.tile([P, 128 * PACK], BF16, name="z%d" % a, align_bytes=64)
                nc.vector.tensor_tensor(
                    z[:].rearrange("p (c i t) -> p c t i", i=2, t=PACK),
                    upper_all[:, :, cols].rearrange("p t (c i) -> p c t i", i=2),
                    w3_raw[:, :, cols].rearrange("p t (c i) -> p c t i", i=2),
                    ALU.subtract,
                )
                part = slice(a - lo, a - lo + 128)
                nc.vector.quantize_mx(out=z_codes[:, part].bitcast(FP8X4), scales=z_scales[:, part], in_=z[:])
            z_q.append((z_codes, z_scales))
        for c, (lo, hi) in enumerate(CHUNKS):
            open_chunk(c)
            z_codes, z_scales = z_q[c]
            for t in range(PACK):
                cols = slice(t * P, (t + 1) * P)
                nc.tensor.matmul_mx(out=h_acc[c, t][:, 0 : hi - lo], lhsT=w2_codes[:, cols].bitcast(FP8X4), lhsT_scale=w2_scales[:, cols],
                                    rhs=z_codes[:].bitcast(FP8X4), rhs_scale=z_scales[:], start=False, stop=True)
            empty_chunk(c)

        out_view = out.rearrange("(p t) j -> p t j", t=PACK)
        for t in range(PACK):
            pair = [keep.tile([P, S], F32, name="pair%d_%d" % (t, i)) for i in range(2)]
            top = keep.tile([P, S], F32, name="top%d" % t)
            res = keep.tile([P, S], F32, name="res%d" % t)
            last = t == PACK - 1
            for c, (a, b) in enumerate(HALVES):
                gather((c, t, 0) in V_SECOND, pair[0][:, a:b], h_win[t][:], second_lists[0][:, a // 16 : b // 16])
            nc.vector.tensor_tensor(top[:], h_win[t][:], pair[0][:], ALU.max)
            for c, (a, b) in enumerate(CHUNKS if last else HALVES):
                gather((c, t, 1) in V_SECOND, pair[1][:, a:b], h_win[t][:], second_lists[1][:, a // 16 : b // 16])
            for lo, hi in CHUNKS if last else ((0, S),):
                nc.vector.tensor_tensor(res[:, lo:hi], top[:, lo:hi], pair[1][:, lo:hi], ALU.min)
                nc.sync.dma_start(out_view[:, t, lo:hi], res[:, lo:hi])
